import numpy as np
import ml_dtypes


def mxq(x, axis, fmt="e4m3"):
    dtype, down = {"e4m3": (ml_dtypes.float8_e4m3fn, 7), "e5m2": (ml_dtypes.float8_e5m2, 14)}[fmt]
    v = np.moveaxis(np.asarray(x, np.float32).astype(ml_dtypes.bfloat16).astype(np.float64), axis, -1)
    blocks = v.reshape(v.shape[:-1] + (-1, 32))
    amax = np.abs(blocks).max(-1, keepdims=True)
    byte = np.maximum(np.where(amax > 0, np.frexp(amax)[1] - 1 + 127, 0) - down, 1)
    scale = np.exp2(byte - 127.0)
    codes = (blocks / scale).astype(np.float32).astype(dtype).astype(np.float64)
    return np.moveaxis((codes * scale).reshape(v.shape), -1, axis)


WIDE = False


def mx_kscale(k):
    if not WIDE:
        return np.ones(k)
    levels = np.array([10, -10, 5, -5, 0])
    if k % 512:
        return np.exp2(np.random.permutation(np.resize(levels, k // 32))).repeat(32)
    a = np.empty((k // 512, 16))
    for p in range(k // 512):
        a[p, :8] = np.random.permutation(np.resize(levels, 8))
        for g in range(8):
            far = levels[np.abs(levels - a[p, g]) >= 10]
            a[p, g + 8] = far[np.random.randint(len(far))]
    return np.exp2(a.ravel()).repeat(32)


def f64(x):
    return np.asarray(x).astype(np.float64)


def striped(idx):
    return np.tile(idx.reshape(-1, 16).T, (8, 1)).astype(np.uint16)


def unstriped(offs):
    return offs[:16].T.reshape(-1).astype(np.int64)


E2M1 = np.array([0.0, 0.5, 1.0, 1.5, 2.0, 3.0, 4.0, 6.0, -0.0, -0.5, -1.0, -1.5, -2.0, -3.0, -4.0, -6.0])


def pack_weight(w, fmt):
    k, n = w.shape
    w = f64(np.asarray(w, np.float32).astype(ml_dtypes.bfloat16)).reshape(k // 32, 32, n)
    amax = np.abs(w).max(1)
    if fmt == "e4m3":
        byte = np.frexp(amax)[1] - 1 + 127 - 7
    else:
        mant, ex = np.frexp(amax / 6.0)
        byte = np.where(mant > 0.5, ex, ex - 1) + 127
    byte = np.clip(np.where(amax > 0, byte, 1), 1, 254)
    scaled = (w * np.exp2(127.0 - byte)[:, None, :]).reshape(k, n).astype(np.float32)
    by_word = np.ascontiguousarray(scaled.reshape(k // 512, 128, 4, n).transpose(0, 1, 3, 2))
    if fmt == "e4m3":
        words = by_word.astype(ml_dtypes.float8_e4m3fn).view(np.uint8)
    else:
        c = by_word.astype(ml_dtypes.float4_e2m1fn).view(np.uint8) & 0xF
        words = (c[..., 0::2] | (c[..., 1::2] << 4)).reshape(k // 512, 128, 2 * n)
    return np.ascontiguousarray(words), np.ascontiguousarray(byte.astype(np.uint8).reshape(k // 512, 16, n))


def unpack_weight(words, scales, fmt):
    g, _, n = scales.shape
    words = np.ascontiguousarray(words).reshape(g, 128, n, -1)
    if fmt == "e4m3":
        vals = words.view(ml_dtypes.float8_e4m3fn).astype(np.float64)
    else:
        nib = np.empty((g, 128, n, 4), np.uint8)
        nib[..., 0::2] = words & 0xF
        nib[..., 1::2] = words >> 4
        vals = E2M1[nib]
    vals = vals * np.repeat(np.exp2(scales.astype(np.float64) - 127.0), 8, axis=1)[..., None]
    return vals.transpose(0, 1, 3, 2).reshape(g * 512, n)


def gelu(v):
    return 0.5 * v * (1.0 + np.tanh(np.sqrt(2.0 / np.pi) * (v + 0.044715 * v**3)))


K, K2, T, T2, S, P, H, N = 1024, 512, 4096, 2048, 1024, 512, 512, 384


def setup_inputs():
    n = np.random.standard_normal
    s = mx_kscale(K)[:, None]
    s2 = mx_kscale(K2)[:, None]
    u = mx_kscale(H)[:, None]
    d = {}
    d["tab_words"], d["tab_scales"] = pack_weight(n((K, T)) * s, "e4m3")
    d["tab2_words"], d["tab2_scales"] = pack_weight(n((K2, T2)) * s2, "e4m3")
    d["offs"] = striped(np.random.permutation(T)[:S])
    d["offs2"] = striped(np.random.permutation(T2)[:P])
    d["pos1"] = striped(np.random.permutation(S)[:P])
    d["w1"] = (0.55 * n((K, H)) / K ** 0.5 / s).astype(np.float32)
    d["gain"] = (np.random.uniform(0.6, 1.4, H) * u[:, 0]).astype(np.float32)
    d["w2_words"], d["w2_scales"] = pack_weight(n((K2, H)) / K2 ** 0.5 / s2 * u.T, "e2m1")
    d["wgs"] = np.exp(0.3 * n((128, P))).astype(np.float32)
    d["gm"] = n((H, S)).astype(np.float32)
    d["w4"] = (n((H, N)) / H ** 0.5 / u).astype(np.float32)
    d["w5_words"], d["w5_scales"] = pack_weight(n((H, N)) / H ** 0.5 / u, "e4m3")
    d["w6"] = (n((H, N)) / H ** 0.5 / u).astype(np.float32)
    return d


def reference(tab_words, tab_scales, tab2_words, tab2_scales, offs, offs2, pos1, w1, gain,
              w2_words, w2_scales, wgs, gm, w4, w5_words, w5_scales, w6):
    v = unpack_weight(tab_words, tab_scales, "e4m3")[:, unstriped(offs)]
    v2 = unpack_weight(tab2_words, tab2_scales, "e4m3")[:, unstriped(offs2)]
    w2 = unpack_weight(w2_words, w2_scales, "e2m1")
    w5 = unpack_weight(w5_words, w5_scales, "e4m3")
    a = np.cos(mxq(f64(w1), 0, "e4m3").T @ v) * f64(gain)[:, None]
    b = np.abs(w2.T @ v2)
    placed = np.zeros((H, S))
    placed[:, unstriped(pos1)] = np.tile(f64(wgs), (H // 128, 1)) * b
    z = a + placed * f64(gm)
    zq = mxq(z, 0, "e4m3")
    y1 = mxq(f64(w4), 0, "e4m3").T @ zq
    y2 = w5.T @ zq
    y3 = mxq(f64(w6), 0, "e4m3").T @ zq
    return y1 * y2 + y3

@@ -1,0 +1,273 @@
+import math
+from contextlib import ExitStack
+
+import concourse.mybir as mybir
+
+K, K2, T, T2, S, SAMPLES, H, N = 1024, 512, 4096, 2048, 1024, 512, 512, 384
+FLOPS = 2 * (K * H * S + K2 * H * SAMPLES + 3 * H * N * S)
+
+F32 = mybir.dt.float32
+BF16 = mybir.dt.bfloat16
+I32 = mybir.dt.int32
+U32 = mybir.dt.uint32
+U16 = mybir.dt.uint16
+U8 = mybir.dt.uint8
+FP8X4 = mybir.dt.float8_e4m3fn_x4
+FP4X4 = mybir.dt.float4_e2m1fn_x4
+ALU = mybir.AluOpType
+ACT = mybir.ActivationFunctionType
+
+P = 128
+PACK = 4
+QUADS = 4
+PASSES = K // (P * PACK)
+HALF = 512
+CHUNK = 256
+
+
+def tile_list_trap_string_landings_kernel(
+    tc, tab_words, tab_scales, tab2_words, tab2_scales, offs, offs2, pos1, w1, gain,
+    w2_words, w2_scales, wgs, gm, w4, w5_words, w5_scales, w6, out,
+):
+    nc = tc.nc
+    with ExitStack() as ctx:
+        lists = ctx.enter_context(tc.tile_pool(name="lists", bufs=1))
+        keep = ctx.enter_context(tc.tile_pool(name="keep", bufs=1))
+        ring = ctx.enter_context(tc.tile_pool(name="ring", bufs=3))
+        psum = ctx.enter_context(tc.psum_pool(name="psum", bufs=1))
+
+        def held(shape, dtype, name):
+            return keep.tile(shape, dtype, name=name, align_bytes=64)
+
+        def load_words(words, name):
+            tile = held([P, words.shape[1]], I32, name)
+            nc.sync.dma_start(tile[:], words.rearrange("p c i -> p (c i)").bitcast(I32))
+            return tile
+
+        def load_scale_rows(tile, scales, quad):
+            rows = scales.shape[0] * 4
+            nc.sync.dma_start(
+                tile[32 * quad : 32 * quad + rows, :].bitcast(I32),
+                scales[:, 4 * quad : 4 * quad + 4, :].bitcast(I32),
+            )
+
+        def load_list(src, name):
+            tile = lists.tile(list(src.shape), U16, name=name)
+            nc.sync.dma_start(tile[:], src)
+            return tile
+
+        tab2_planes = held([P, T2], U8, "tab2_planes")
+        w2_planes = held([P, H], U8, "w2_planes")
+        tab_planes = held([P, T], U8, "tab_planes")
+        w5_planes = held([P, N], U8, "w5_planes")
+        seed = held([P, 16], F32, "seed")
+        nc.vector.memset(seed[:], 0.0)
+        for planes in (tab2_planes, w2_planes, tab_planes):
+            nc.vector.memset(planes[:].bitcast(I32), 0)
+        pages = [held([P, S], F32, "page%d" % t) for t in range(PACK)]
+        for page in pages:
+            nc.gpsimd.memset(page[:], 0.0)
+        nc.gpsimd.memset(w5_planes[:].bitcast(I32), 0)
+
+        warm = held([P, 16], F32, "warm")
+        nc.scalar.activation(warm[:], seed[:], ACT.Sin)
+
+        def load_wgs(u):
+            tile = held([P, 2, SAMPLES], F32, "wgs%d" % u)
+            for quad in (0, 2, 1, 3):
+                nc.sync.dma_start(
+                    tile[32 * quad : 32 * quad + 32],
+                    wgs.rearrange("(q t) j -> q t j", t=PACK)[:, 2 * u : 2 * u + 2, :],
+                )
+            return tile
+
+        def load_w1(a):
+            raw = held([P, PACK, H], F32, "w1_raw%d" % a)
+            nc.sync.dma_start(raw[:], w1[512 * a : 512 * (a + 1), :].rearrange("(p i) c -> p i c", i=PACK))
+            return raw
+
+        idx2 = load_list(offs2, "idx2")
+        w2_raw = held([P, 2 * H], U8, "w2_raw")
+        nc.sync.dma_start(w2_raw[:].bitcast(I32), w2_words[0].bitcast(I32))
+        for quad in range(QUADS):
+            load_scale_rows(tab2_planes, tab2_scales, quad)
+        tab2_sb = load_words(tab2_words[0], "tab2_sb")
+        for quad in range(QUADS):
+            load_scale_rows(w2_planes, w2_scales, quad)
+        idx = load_list(offs, "idx")
+        for quad in range(QUADS):
+            load_scale_rows(tab_planes, tab_scales, quad)
+        places = load_list(pos1, "places")
+        wgs_sb = [load_wgs(0)]
+        w1_raw = [load_w1(a) for a in range(PASSES)]
+        tab_sb = [load_words(tab_words[a], "tab_sb%d" % a) for a in range(PASSES)]
+        wgs_sb.append(load_wgs(1))
+        gain_sb = held([P, PACK], F32, "gain_sb")
+        nc.sync.dma_start(gain_sb[:], gain.rearrange("(p t) -> p t", t=PACK))
+        w46_raw = []
+        for name, w in (("w4_raw", w4), ("w6_raw", w6)):
+            raw = held([P, PACK, N], F32, name)
+            nc.sync.dma_start(raw[:], w.rearrange("(p i) c -> p i c", i=PACK))
+            w46_raw.append(raw)
+        gm_sb = []
+        for t in range(PACK):
+            g = held([P, S], F32, "gm%d" % t)
+            nc.sync.dma_start(g[:], gm.rearrange("(p t) j -> p t j", t=PACK)[:, t, :])
+            gm_sb.append(g)
+        w5_sb = load_words(w5_words[0], "w5_sb")
+        for quad in range(QUADS):
+            load_scale_rows(w5_planes, w5_scales, quad)
+
+        v2_planes = held([P, SAMPLES], U8, "v2_planes")
+        nc.vector.tensor_copy(v2_planes[:], tab2_planes[:].indirect(idx2[:]))
+        w2_codes = held([P, 2 * H], U8, "w2_codes")
+        nc.vector.tensor_copy(
+            w2_codes[:].rearrange("p (t m e) -> p t m e", t=PACK, e=2),
+            w2_raw[:].rearrange("p (m t e) -> p t m e", t=PACK, e=2),
+        )
+        v2_codes = held([P, SAMPLES], U32, "v2_codes")
+        nc.vector.tensor_copy(v2_codes[:], tab2_sb[:].bitcast(U32).indirect(idx2[:]))
+        w2_dealt = held([P, H], U8, "w2_dealt")
+        nc.vector.tensor_copy(
+            w2_dealt[:].rearrange("p (t m) -> p t m", t=PACK),
+            w2_planes[:].rearrange("p (m t) -> p t m", t=PACK),
+        )
+        b_sizes = []
+        for t in range(PACK):
+            acc = psum.tile([P, SAMPLES], F32, name="acc", tag="acc", bufs=3)
+            nc.tensor.matmul_mx(
+                out=acc[:],
+                lhsT=w2_codes[:, 2 * P * t : 2 * P * (t + 1)].bitcast(FP4X4),
+                lhsT_scale=w2_dealt[:, P * t : P * (t + 1)],
+                rhs=v2_codes[:].bitcast(FP8X4),
+                rhs_scale=v2_planes[:],
+                start=True,
+                stop=True,
+            )
+            b_abs = held([P, SAMPLES], F32, "b_abs%d" % t)
+            nc.scalar.activation(b_abs[:], acc[:], ACT.Abs)
+            b_sizes.append(b_abs)
+
+        def place(t):
+            nc.vector.tensor_tensor(
+                pages[t][:].indirect(places[:]), b_sizes[t][:], wgs_sb[t // 2][:, t % 2, :], ALU.mult
+            )
+
+        place(0)
+        place(1)
+
+        w1_codes, w1_planes = [], []
+        for a in range(PASSES):
+            grouped = held([P, H * PACK], BF16, "w1_grouped%d" % a)
+            nc.scalar.copy(
+                grouped[:].rearrange("p (t m i) -> p m t i", t=PACK, i=PACK),
+                w1_raw[a][:].rearrange("p i (m t) -> p m t i", t=PACK),
+            )
+            codes = held([P, H], U32, "w1_codes%d" % a)
+            planes = held([P, H], U8, "w1_planes%d" % a)
+            nc.vector.quantize_mx(out=codes[:].bitcast(FP8X4), scales=planes[:], in_=grouped[:])
+            w1_codes.append(codes)
+            w1_planes.append(planes)
+
+        cosines = {}
+        for h in range(S // HALF):
+            part = idx[:, h * HALF // 16 : (h + 1) * HALF // 16]
+            v_planes = held([P, HALF], U8, "v_planes%d" % h)
+            nc.vector.tensor_copy(v_planes[:], tab_planes[:].indirect(part))
+            v_codes = []
+            for a in range(PASSES):
+                codes = held([P, HALF], U32, "v_codes%d_%d" % (h, a))
+                nc.vector.tensor_copy(codes[:], tab_sb[a][:].bitcast(U32).indirect(part))
+                v_codes.append(codes)
+            for t in range(PACK):
+                acc = psum.tile([P, HALF], F32, name="acc", tag="acc", bufs=3)
+                for a in range(PASSES):
+                    nc.tensor.matmul_mx(
+                        out=acc[:],
+                        lhsT=w1_codes[a][:, P * t : P * (t + 1)].bitcast(FP8X4),
+                        lhsT_scale=w1_planes[a][:, P * t : P * (t + 1)],
+                        rhs=v_codes[a][:].bitcast(FP8X4),
+                        rhs_scale=v_planes[4 * a : P, :],
+                        start=(a == 0),
+                        stop=(a == PASSES - 1),
+                    )
+                size = ring.tile([P, HALF], F32, name="size")
+                nc.scalar.activation(size[:], acc[:], ACT.Abs)
+                cosine = held([P, HALF], F32, "cos%d_%d" % (h, t))
+                nc.scalar.activation(cosine[:], size[:], ACT.Sin, bias=math.pi / 2, scale=-1.0)
+                cosines[h, t] = cosine
+
+        place(2)
+        place(3)
+
+        w46_grouped = held([P, 2 * N, PACK], BF16, "w46_grouped")
+        for u in range(2):
+            nc.scalar.copy(w46_grouped[:, N * u : N * (u + 1), :], w46_raw[u][:].rearrange("p i c -> p c i"))
+        w46_codes = held([P, 2 * N], U32, "w46_codes")
+        w46_planes = held([P, 2 * N], U8, "w46_planes")
+        for c0, c1 in ((0, 512), (512, 2 * N)):
+            nc.vector.quantize_mx(
+                out=w46_codes[:, c0:c1].bitcast(FP8X4),
+                scales=w46_planes[:, c0:c1],
+                in_=w46_grouped[:, c0:c1, :].rearrange("p c i -> p (c i)"),
+            )
+
+        gated = []
+        for t in range(PACK):
+            nc.vector.tensor_tensor(gm_sb[t][:], pages[t][:], gm_sb[t][:], ALU.mult)
+            gated.append(gm_sb[t])
+
+        chunks = S // CHUNK
+        z_rows, z_grouped, z_q = {}, {}, {}
+
+        def make_z(c):
+            h, c0 = divmod(c * CHUNK, HALF)
+            rows = ring.tile([P, PACK, CHUNK], BF16, name="z_rows")
+            for t in range(PACK):
+                nc.vector.scalar_tensor_tensor(
+                    rows[:, t, :], cosines[h, t][:, c0 : c0 + CHUNK], gain_sb[:, t : t + 1],
+                    gated[t][:, c * CHUNK : (c + 1) * CHUNK], ALU.mult, ALU.add,
+                )
+            grouped = ring.tile([P, CHUNK, PACK], BF16, name="z_grouped", align_bytes=64)
+            nc.scalar.copy(grouped[:], rows[:].rearrange("p t c -> p c t"))
+            z_grouped[c] = grouped
+
+        def quantise_z(c):
+            codes = ring.tile([P, CHUNK], U32, name="z_codes", align_bytes=64)
+            planes = ring.tile([P, CHUNK], U8, name="z_planes", align_bytes=64)
+            nc.vector.quantize_mx(
+                out=codes[:].bitcast(FP8X4), scales=planes[:], in_=z_grouped[c][:].rearrange("p c t -> p (c t)")
+            )
+            z_q[c] = (codes, planes)
+
+        def finish(c):
+            codes, planes = z_q[c]
+            for n in range(N // P):
+                y13 = psum.tile([P, 2, CHUNK], F32, name="y13", tag="y13", bufs=3)
+                y2 = psum.tile([P, CHUNK], F32, name="y2", tag="y2", bufs=2)
+                cols = slice(P * n, P * (n + 1))
+                cols6 = slice(N + P * n, N + P * (n + 1))
+                for dst, w_codes, w_planes in (
+                    (y2[:], w5_sb[:, cols], w5_planes[:, cols]),
+                    (y13[:, 0, :], w46_codes[:, cols], w46_planes[:, cols]),
+                    (y13[:, 1, :], w46_codes[:, cols6], w46_planes[:, cols6]),
+                ):
+                    nc.tensor.matmul_mx(
+                        out=dst, lhsT=w_codes.bitcast(FP8X4), lhsT_scale=w_planes,
+                        rhs=codes[:].bitcast(FP8X4), rhs_scale=planes[:], start=True, stop=True,
+                    )
+                y2_sb = ring.tile([P, CHUNK], F32, name="y2_sb")
+                nc.scalar.copy(y2_sb[:], y2[:])
+                prod = ring.tile([P, CHUNK], F32, name="prod")
+                nc.vector.tensor_tensor(prod[:], y13[:, 0, :], y2_sb[:], ALU.mult)
+                res = ring.tile([P, CHUNK], F32, name="res", bufs=6)
+                nc.vector.tensor_tensor(res[:], y13[:, 1, :], prod[:], ALU.add)
+                nc.sync.dma_start(out[cols, c * CHUNK : (c + 1) * CHUNK], res[:])
+
+        for step in range(chunks + 2):
+            if step < chunks:
+                make_z(step)
+            if 1 <= step <= chunks:
+                quantise_z(step - 1)
+            if step >= 2:
+                finish(step - 2)

@@ -22,7 +22,8 @@ PACK = 4
 QUADS = 4
 PASSES = K // (P * PACK)
 HALF = 512
-CHUNK = 256
+CHUNKS = (256, 256, 256, 128, 128)
+EARLY = 3
 
 
 def tile_list_trap_string_landings_kernel(
@@ -58,57 +59,53 @@ def tile_list_trap_string_landings_kernel(
 
         tab2_planes = held([P, T2], U8, "tab2_planes")
         w2_planes = held([P, H], U8, "w2_planes")
-        tab_planes = held([P, T], U8, "tab_planes")
+        tab_rows = held([P, T], U8, "tab_rows")
         w5_planes = held([P, N], U8, "w5_planes")
-        seed = held([P, 16], F32, "seed")
-        nc.vector.memset(seed[:], 0.0)
-        for planes in (tab2_planes, w2_planes, tab_planes):
-            nc.vector.memset(planes[:].bitcast(I32), 0)
+        v_planes = held([P, S], U8, "v_planes")
         pages = [held([P, S], F32, "page%d" % t) for t in range(PACK)]
+        for planes in (tab2_planes, w2_planes, tab_rows):
+            nc.gpsimd.memset(planes[:].bitcast(I32), 0)
         for page in pages:
             nc.gpsimd.memset(page[:], 0.0)
-        nc.gpsimd.memset(w5_planes[:].bitcast(I32), 0)
-
+        for planes in (v_planes, w5_planes):
+            nc.gpsimd.memset(planes[:].bitcast(I32), 0)
+        seed = held([P, 16], F32, "seed")
+        nc.vector.memset(seed[:], 0.0)
         warm = held([P, 16], F32, "warm")
         nc.scalar.activation(warm[:], seed[:], ACT.Sin)
 
-        def load_wgs(u):
-            tile = held([P, 2, SAMPLES], F32, "wgs%d" % u)
+        def load_wgs(t0, t1):
+            tile = held([P, t1 - t0, SAMPLES], F32, "wgs%d" % t0)
             for quad in (0, 2, 1, 3):
                 nc.sync.dma_start(
                     tile[32 * quad : 32 * quad + 32],
-                    wgs.rearrange("(q t) j -> q t j", t=PACK)[:, 2 * u : 2 * u + 2, :],
+                    wgs.rearrange("(q t) j -> q t j", t=PACK)[:, t0:t1, :],
                 )
-            return tile
+            return [tile[:, t, :] for t in range(t1 - t0)]
 
-        def load_w1(a):
-            raw = held([P, PACK, H], F32, "w1_raw%d" % a)
-            nc.sync.dma_start(raw[:], w1[512 * a : 512 * (a + 1), :].rearrange("(p i) c -> p i c", i=PACK))
+        def load_rows(w, name):
+            raw = held([P, PACK, w.shape[1]], F32, name)
+            nc.sync.dma_start(raw[:], w.rearrange("(p i) c -> p i c", i=PACK))
             return raw
 
         idx2 = load_list(offs2, "idx2")
         w2_raw = held([P, 2 * H], U8, "w2_raw")
         nc.sync.dma_start(w2_raw[:].bitcast(I32), w2_words[0].bitcast(I32))
-        for quad in range(QUADS):
+        places = load_list(pos1, "places")
+        for quad in (0, 2, 1, 3):
             load_scale_rows(tab2_planes, tab2_scales, quad)
         tab2_sb = load_words(tab2_words[0], "tab2_sb")
-        for quad in range(QUADS):
+        for quad in (0, 2, 1, 3):
             load_scale_rows(w2_planes, w2_scales, quad)
         idx = load_list(offs, "idx")
-        for quad in range(QUADS):
-            load_scale_rows(tab_planes, tab_scales, quad)
-        places = load_list(pos1, "places")
-        wgs_sb = [load_wgs(0)]
-        w1_raw = [load_w1(a) for a in range(PASSES)]
+        nc.sync.dma_start(tab_rows[0:32, :].bitcast(I32), tab_scales.rearrange("a q t -> (a q) t").bitcast(I32))
+        wgs_sb = load_wgs(0, EARLY)
+        w1_raw = [load_rows(w1[512 * a : 512 * (a + 1), :], "w1_raw%d" % a) for a in range(PASSES)]
+        w46_raw = [load_rows(w4, "w4_raw"), load_rows(w6, "w6_raw")]
         tab_sb = [load_words(tab_words[a], "tab_sb%d" % a) for a in range(PASSES)]
-        wgs_sb.append(load_wgs(1))
+        wgs_sb.extend(load_wgs(EARLY, PACK))
         gain_sb = held([P, PACK], F32, "gain_sb")
         nc.sync.dma_start(gain_sb[:], gain.rearrange("(p t) -> p t", t=PACK))
-        w46_raw = []
-        for name, w in (("w4_raw", w4), ("w6_raw", w6)):
-            raw = held([P, PACK, N], F32, name)
-            nc.sync.dma_start(raw[:], w.rearrange("(p i) c -> p i c", i=PACK))
-            w46_raw.append(raw)
         gm_sb = []
         for t in range(PACK):
             g = held([P, S], F32, "gm%d" % t)
@@ -132,6 +129,14 @@ def tile_list_trap_string_landings_kernel(
             w2_dealt[:].rearrange("p (t m) -> p t m", t=PACK),
             w2_planes[:].rearrange("p (m t) -> p t m", t=PACK),
         )
+        v_rows = held([P, S], U8, "v_rows")
+        nc.vector.tensor_copy(v_rows[:], tab_rows[:].indirect(idx[:]))
+        for a in range(PASSES):
+            for quad in range(QUADS):
+                nc.gpsimd.dma_start(
+                    v_planes[32 * quad + 4 * a : 32 * quad + 4 * a + 4, :].bitcast(I32),
+                    v_rows[16 * a + 4 * quad : 16 * a + 4 * quad + 4, :].bitcast(I32),
+                )
         b_sizes = []
         for t in range(PACK):
             acc = psum.tile([P, SAMPLES], F32, name="acc", tag="acc", bufs=3)
@@ -150,11 +155,11 @@ def tile_list_trap_string_landings_kernel(
 
         def place(t):
             nc.vector.tensor_tensor(
-                pages[t][:].indirect(places[:]), b_sizes[t][:], wgs_sb[t // 2][:, t % 2, :], ALU.mult
+                pages[t][:].indirect(places[:]), b_sizes[t][:], wgs_sb[t], ALU.mult
             )
 
-        place(0)
-        place(1)
+        for t in range(EARLY):
+            place(t)
 
         w1_codes, w1_planes = [], []
         for a in range(PASSES):
@@ -169,11 +174,21 @@ def tile_list_trap_string_landings_kernel(
             w1_codes.append(codes)
             w1_planes.append(planes)
 
+        w46_grouped = held([P, 2 * N, PACK], BF16, "w46_grouped")
+        for u in range(2):
+            nc.scalar.copy(w46_grouped[:, N * u : N * (u + 1), :], w46_raw[u][:].rearrange("p i c -> p c i"))
+        w46_codes = held([P, 2 * N], U32, "w46_codes")
+        w46_planes = held([P, 2 * N], U8, "w46_planes")
+        for c0, c1 in ((0, 512), (512, 2 * N)):
+            nc.vector.quantize_mx(
+                out=w46_codes[:, c0:c1].bitcast(FP8X4),
+                scales=w46_planes[:, c0:c1],
+                in_=w46_grouped[:, c0:c1, :].rearrange("p c i -> p (c i)"),
+            )
+
         cosines = {}
         for h in range(S // HALF):
             part = idx[:, h * HALF // 16 : (h + 1) * HALF // 16]
-            v_planes = held([P, HALF], U8, "v_planes%d" % h)
-            nc.vector.tensor_copy(v_planes[:], tab_planes[:].indirect(part))
             v_codes = []
             for a in range(PASSES):
                 codes = held([P, HALF], U32, "v_codes%d_%d" % (h, a))
@@ -187,7 +202,7 @@ def tile_list_trap_string_landings_kernel(
                         lhsT=w1_codes[a][:, P * t : P * (t + 1)].bitcast(FP8X4),
                         lhsT_scale=w1_planes[a][:, P * t : P * (t + 1)],
                         rhs=v_codes[a][:].bitcast(FP8X4),
-                        rhs_scale=v_planes[4 * a : P, :],
+                        rhs_scale=v_planes[4 * a : P, h * HALF : (h + 1) * HALF],
                         start=(a == 0),
                         stop=(a == PASSES - 1),
                     )
@@ -197,77 +212,80 @@ def tile_list_trap_string_landings_kernel(
                 nc.scalar.activation(cosine[:], size[:], ACT.Sin, bias=math.pi / 2, scale=-1.0)
                 cosines[h, t] = cosine
 
-        place(2)
-        place(3)
-
-        w46_grouped = held([P, 2 * N, PACK], BF16, "w46_grouped")
-        for u in range(2):
-            nc.scalar.copy(w46_grouped[:, N * u : N * (u + 1), :], w46_raw[u][:].rearrange("p i c -> p c i"))
-        w46_codes = held([P, 2 * N], U32, "w46_codes")
-        w46_planes = held([P, 2 * N], U8, "w46_planes")
-        for c0, c1 in ((0, 512), (512, 2 * N)):
-            nc.vector.quantize_mx(
-                out=w46_codes[:, c0:c1].bitcast(FP8X4),
-                scales=w46_planes[:, c0:c1],
-                in_=w46_grouped[:, c0:c1, :].rearrange("p c i -> p (c i)"),
-            )
+        for t in range(EARLY, PACK):
+            place(t)
 
         gated = []
         for t in range(PACK):
             nc.vector.tensor_tensor(gm_sb[t][:], pages[t][:], gm_sb[t][:], ALU.mult)
             gated.append(gm_sb[t])
 
-        chunks = S // CHUNK
-        z_rows, z_grouped, z_q = {}, {}, {}
+        starts = [sum(CHUNKS[:c]) for c in range(len(CHUNKS))]
+        z_grouped, z_q = {}, {}
 
         def make_z(c):
-            h, c0 = divmod(c * CHUNK, HALF)
-            rows = ring.tile([P, PACK, CHUNK], BF16, name="z_rows")
+            width = CHUNKS[c]
+            h, c0 = divmod(starts[c], HALF)
+            rows = ring.tile([P, PACK, width], BF16, name="z_rows")
             for t in range(PACK):
                 nc.vector.scalar_tensor_tensor(
-                    rows[:, t, :], cosines[h, t][:, c0 : c0 + CHUNK], gain_sb[:, t : t + 1],
-                    gated[t][:, c * CHUNK : (c + 1) * CHUNK], ALU.mult, ALU.add,
+                    rows[:, t, :], cosines[h, t][:, c0 : c0 + width], gain_sb[:, t : t + 1],
+                    gated[t][:, starts[c] : starts[c] + width], ALU.mult, ALU.add,
                 )
-            grouped = ring.tile([P, CHUNK, PACK], BF16, name="z_grouped", align_bytes=64)
+            grouped = ring.tile([P, width, PACK], BF16, name="z_grouped", align_bytes=64)
             nc.scalar.copy(grouped[:], rows[:].rearrange("p t c -> p c t"))
             z_grouped[c] = grouped
 
         def quantise_z(c):
-            codes = ring.tile([P, CHUNK], U32, name="z_codes", align_bytes=64)
-            planes = ring.tile([P, CHUNK], U8, name="z_planes", align_bytes=64)
+            codes = ring.tile([P, CHUNKS[c]], U32, name="z_codes", align_bytes=64)
+            planes = ring.tile([P, CHUNKS[c]], U8, name="z_planes", align_bytes=64)
             nc.vector.quantize_mx(
                 out=codes[:].bitcast(FP8X4), scales=planes[:], in_=z_grouped[c][:].rearrange("p c t -> p (c t)")
             )
             z_q[c] = (codes, planes)
 
         def finish(c):
+            width = CHUNKS[c]
             codes, planes = z_q[c]
-            for n in range(N // P):
-                y13 = psum.tile([P, 2, CHUNK], F32, name="y13", tag="y13", bufs=3)
-                y2 = psum.tile([P, CHUNK], F32, name="y2", tag="y2", bufs=2)
+            y13, prod = [], []
+
+            def multiply(n):
+                pair = psum.tile([P, 2, width], F32, name="y13", tag="y13", bufs=3)
+                y2 = psum.tile([P, width], F32, name="y2", tag="y2", bufs=2)
                 cols = slice(P * n, P * (n + 1))
                 cols6 = slice(N + P * n, N + P * (n + 1))
                 for dst, w_codes, w_planes in (
                     (y2[:], w5_sb[:, cols], w5_planes[:, cols]),
-                    (y13[:, 0, :], w46_codes[:, cols], w46_planes[:, cols]),
-                    (y13[:, 1, :], w46_codes[:, cols6], w46_planes[:, cols6]),
+                    (pair[:, 0, :], w46_codes[:, cols], w46_planes[:, cols]),
+                    (pair[:, 1, :], w46_codes[:, cols6], w46_planes[:, cols6]),
                 ):
                     nc.tensor.matmul_mx(
                         out=dst, lhsT=w_codes.bitcast(FP8X4), lhsT_scale=w_planes,
                         rhs=codes[:].bitcast(FP8X4), rhs_scale=planes[:], start=True, stop=True,
                     )
-                y2_sb = ring.tile([P, CHUNK], F32, name="y2_sb")
+                y2_sb = ring.tile([P, width], F32, name="y2_sb")
                 nc.scalar.copy(y2_sb[:], y2[:])
-                prod = ring.tile([P, CHUNK], F32, name="prod")
-                nc.vector.tensor_tensor(prod[:], y13[:, 0, :], y2_sb[:], ALU.mult)
-                res = ring.tile([P, CHUNK], F32, name="res", bufs=6)
-                nc.vector.tensor_tensor(res[:], y13[:, 1, :], prod[:], ALU.add)
-                nc.sync.dma_start(out[cols, c * CHUNK : (c + 1) * CHUNK], res[:])
+                y12 = ring.tile([P, width], F32, name="y12")
+                nc.vector.tensor_tensor(y12[:], pair[:, 0, :], y2_sb[:], ALU.mult)
+                y13.append(pair)
+                prod.append(y12)
 
-        for step in range(chunks + 2):
-            if step < chunks:
+            def add_and_store(n):
+                res = ring.tile([P, width], F32, name="res", bufs=6)
+                nc.vector.tensor_tensor(res[:], y13[n][:, 1, :], prod[n][:], ALU.add)
+                nc.sync.dma_start(out[P * n : P * (n + 1), starts[c] : starts[c] + width], res[:])
+
+            tiles = N // P
+            for n in range(tiles + 1):
+                if n < tiles:
+                    multiply(n)
+                if n >= 1:
+                    add_and_store(n - 1)
+
+        for step in range(len(CHUNKS) + 2):
+            if step < len(CHUNKS):
                 make_z(step)
-            if 1 <= step <= chunks:
+            if 1 <= step <= len(CHUNKS):
                 quantise_z(step - 1)
             if step >= 2:
                 finish(step - 2)

@@ -22,8 +22,8 @@ PACK = 4
 QUADS = 4
 PASSES = K // (P * PACK)
 HALF = 512
-CHUNKS = (256, 256, 256, 128, 128)
-EARLY = 3
+CHUNKS = (256, 256, 256, 256)
+STRIP = 128
 
 
 def tile_list_trap_string_landings_kernel(
@@ -59,20 +59,21 @@ def tile_list_trap_string_landings_kernel(
 
         tab2_planes = held([P, T2], U8, "tab2_planes")
         w2_planes = held([P, H], U8, "w2_planes")
-        tab_rows = held([P, T], U8, "tab_rows")
+        tab_planes = held([P, T], U8, "tab_planes")
         w5_planes = held([P, N], U8, "w5_planes")
         v_planes = held([P, S], U8, "v_planes")
         pages = [held([P, S], F32, "page%d" % t) for t in range(PACK)]
-        for planes in (tab2_planes, w2_planes, tab_rows):
+        for planes in (tab2_planes, w2_planes, tab_planes):
             nc.gpsimd.memset(planes[:].bitcast(I32), 0)
-        for page in pages:
+        for page in pages[2:]:
             nc.gpsimd.memset(page[:], 0.0)
-        for planes in (v_planes, w5_planes):
-            nc.gpsimd.memset(planes[:].bitcast(I32), 0)
+        nc.gpsimd.memset(w5_planes[:].bitcast(I32), 0)
         seed = held([P, 16], F32, "seed")
         nc.vector.memset(seed[:], 0.0)
         warm = held([P, 16], F32, "warm")
         nc.scalar.activation(warm[:], seed[:], ACT.Sin)
+        for page in pages[:2]:
+            nc.vector.memset(page[:], 0.0)
 
         def load_wgs(t0, t1):
             tile = held([P, t1 - t0, SAMPLES], F32, "wgs%d" % t0)
@@ -91,19 +92,21 @@ def tile_list_trap_string_landings_kernel(
         idx2 = load_list(offs2, "idx2")
         w2_raw = held([P, 2 * H], U8, "w2_raw")
         nc.sync.dma_start(w2_raw[:].bitcast(I32), w2_words[0].bitcast(I32))
-        places = load_list(pos1, "places")
+        idx = load_list(offs, "idx")
         for quad in (0, 2, 1, 3):
             load_scale_rows(tab2_planes, tab2_scales, quad)
         tab2_sb = load_words(tab2_words[0], "tab2_sb")
         for quad in (0, 2, 1, 3):
             load_scale_rows(w2_planes, w2_scales, quad)
-        idx = load_list(offs, "idx")
-        nc.sync.dma_start(tab_rows[0:32, :].bitcast(I32), tab_scales.rearrange("a q t -> (a q) t").bitcast(I32))
-        wgs_sb = load_wgs(0, EARLY)
-        w1_raw = [load_rows(w1[512 * a : 512 * (a + 1), :], "w1_raw%d" % a) for a in range(PASSES)]
+        for quad in (0, 2, 1, 3):
+            load_scale_rows(tab_planes, tab_scales, quad)
+        places = load_list(pos1, "places")
+        wgs_sb, w1_raw = [], []
+        for a in range(PASSES):
+            wgs_sb.extend(load_wgs(2 * a, 2 * a + 2))
+            w1_raw.append(load_rows(w1[512 * a : 512 * (a + 1), :], "w1_raw%d" % a))
         w46_raw = [load_rows(w4, "w4_raw"), load_rows(w6, "w6_raw")]
         tab_sb = [load_words(tab_words[a], "tab_sb%d" % a) for a in range(PASSES)]
-        wgs_sb.extend(load_wgs(EARLY, PACK))
         gain_sb = held([P, PACK], F32, "gain_sb")
         nc.sync.dma_start(gain_sb[:], gain.rearrange("(p t) -> p t", t=PACK))
         gm_sb = []
@@ -129,17 +132,10 @@ def tile_list_trap_string_landings_kernel(
             w2_dealt[:].rearrange("p (t m) -> p t m", t=PACK),
             w2_planes[:].rearrange("p (m t) -> p t m", t=PACK),
         )
-        v_rows = held([P, S], U8, "v_rows")
-        nc.vector.tensor_copy(v_rows[:], tab_rows[:].indirect(idx[:]))
-        for a in range(PASSES):
-            for quad in range(QUADS):
-                nc.gpsimd.dma_start(
-                    v_planes[32 * quad + 4 * a : 32 * quad + 4 * a + 4, :].bitcast(I32),
-                    v_rows[16 * a + 4 * quad : 16 * a + 4 * quad + 4, :].bitcast(I32),
-                )
+        nc.vector.tensor_copy(v_planes[:], tab_planes[:].indirect(idx[:]))
         b_sizes = []
         for t in range(PACK):
-            acc = psum.tile([P, SAMPLES], F32, name="acc", tag="acc", bufs=3)
+            acc = psum.tile([P, SAMPLES], F32, name="acc", tag="bank", bufs=8)
             nc.tensor.matmul_mx(
                 out=acc[:],
                 lhsT=w2_codes[:, 2 * P * t : 2 * P * (t + 1)].bitcast(FP4X4),
@@ -158,7 +154,7 @@ def tile_list_trap_string_landings_kernel(
                 pages[t][:].indirect(places[:]), b_sizes[t][:], wgs_sb[t], ALU.mult
             )
 
-        for t in range(EARLY):
+        for t in range(PACK):
             place(t)
 
         w1_codes, w1_planes = [], []
@@ -187,6 +183,12 @@ def tile_list_trap_string_landings_kernel(
             )
 
         cosines = {}
+
+        def take_cosine(h, t, size):
+            cosine = held([P, HALF], F32, "cos%d_%d" % (h, t))
+            nc.scalar.activation(cosine[:], size[:], ACT.Sin, bias=math.pi / 2, scale=-1.0)
+            cosines[h, t] = cosine
+
         for h in range(S // HALF):
             part = idx[:, h * HALF // 16 : (h + 1) * HALF // 16]
             v_codes = []
@@ -195,7 +197,7 @@ def tile_list_trap_string_landings_kernel(
                 nc.vector.tensor_copy(codes[:], tab_sb[a][:].bitcast(U32).indirect(part))
                 v_codes.append(codes)
             for t in range(PACK):
-                acc = psum.tile([P, HALF], F32, name="acc", tag="acc", bufs=3)
+                acc = psum.tile([P, HALF], F32, name="acc", tag="bank", bufs=8)
                 for a in range(PASSES):
                     nc.tensor.matmul_mx(
                         out=acc[:],
@@ -208,12 +210,10 @@ def tile_list_trap_string_landings_kernel(
                     )
                 size = ring.tile([P, HALF], F32, name="size")
                 nc.scalar.activation(size[:], acc[:], ACT.Abs)
-                cosine = held([P, HALF], F32, "cos%d_%d" % (h, t))
-                nc.scalar.activation(cosine[:], size[:], ACT.Sin, bias=math.pi / 2, scale=-1.0)
-                cosines[h, t] = cosine
-
-        for t in range(EARLY, PACK):
-            place(t)
+                if t > 0:
+                    take_cosine(h, t - 1, last_size)
+                last_size = size
+            take_cosine(h, PACK - 1, last_size)
 
         gated = []
         for t in range(PACK):
@@ -221,71 +221,81 @@ def tile_list_trap_string_landings_kernel(
             gated.append(gm_sb[t])
 
         starts = [sum(CHUNKS[:c]) for c in range(len(CHUNKS))]
-        z_grouped, z_q = {}, {}
+        z_rows, z_grouped, z_q = {}, {}, {}
 
         def make_z(c):
             width = CHUNKS[c]
             h, c0 = divmod(starts[c], HALF)
-            rows = ring.tile([P, PACK, width], BF16, name="z_rows")
+            rows = ring.tile([P, PACK, width], BF16, name="z_rows", bufs=4)
             for t in range(PACK):
                 nc.vector.scalar_tensor_tensor(
                     rows[:, t, :], cosines[h, t][:, c0 : c0 + width], gain_sb[:, t : t + 1],
                     gated[t][:, starts[c] : starts[c] + width], ALU.mult, ALU.add,
                 )
-            grouped = ring.tile([P, width, PACK], BF16, name="z_grouped", align_bytes=64)
-            nc.scalar.copy(grouped[:], rows[:].rearrange("p t c -> p c t"))
+            z_rows[c] = rows
+
+        def interleave_z(c):
+            grouped = ring.tile([P, CHUNKS[c], PACK], BF16, name="z_grouped", align_bytes=64, bufs=4)
+            copy = nc.vector.tensor_copy if starts[c] < HALF else nc.scalar.copy
+            copy(grouped[:], z_rows[c][:].rearrange("p t c -> p c t"))
             z_grouped[c] = grouped
 
         def quantise_z(c):
-            codes = ring.tile([P, CHUNKS[c]], U32, name="z_codes", align_bytes=64)
-            planes = ring.tile([P, CHUNKS[c]], U8, name="z_planes", align_bytes=64)
+            codes = ring.tile([P, CHUNKS[c]], U32, name="z_codes", align_bytes=64, bufs=4)
+            planes = ring.tile([P, CHUNKS[c]], U8, name="z_planes", align_bytes=64, bufs=4)
             nc.vector.quantize_mx(
                 out=codes[:].bitcast(FP8X4), scales=planes[:], in_=z_grouped[c][:].rearrange("p c t -> p (c t)")
             )
             z_q[c] = (codes, planes)
 
-        def finish(c):
-            width = CHUNKS[c]
+        tiles = N // P
+        pending = []
+
+        def multiply(c, c0):
             codes, planes = z_q[c]
-            y13, prod = [], []
-
-            def multiply(n):
-                pair = psum.tile([P, 2, width], F32, name="y13", tag="y13", bufs=3)
-                y2 = psum.tile([P, width], F32, name="y2", tag="y2", bufs=2)
-                cols = slice(P * n, P * (n + 1))
-                cols6 = slice(N + P * n, N + P * (n + 1))
-                for dst, w_codes, w_planes in (
-                    (y2[:], w5_sb[:, cols], w5_planes[:, cols]),
-                    (pair[:, 0, :], w46_codes[:, cols], w46_planes[:, cols]),
-                    (pair[:, 1, :], w46_codes[:, cols6], w46_planes[:, cols6]),
-                ):
+            cols = slice(c0, c0 + STRIP)
+            banks = []
+            for w_codes, w_planes, first in ((w5_sb, w5_planes, 0), (w46_codes, w46_planes, 0), (w46_codes, w46_planes, N)):
+                bank = psum.tile([P, tiles, STRIP], F32, name="y", tag="bank", bufs=8)
+                for n in range(tiles):
+                    w_cols = slice(first + P * n, first + P * (n + 1))
                     nc.tensor.matmul_mx(
-                        out=dst, lhsT=w_codes.bitcast(FP8X4), lhsT_scale=w_planes,
-                        rhs=codes[:].bitcast(FP8X4), rhs_scale=planes[:], start=True, stop=True,
+                        out=bank[:, n, :], lhsT=w_codes[:, w_cols].bitcast(FP8X4), lhsT_scale=w_planes[:, w_cols],
+                        rhs=codes[:, cols].bitcast(FP8X4), rhs_scale=planes[:, cols], start=True, stop=True,
                     )
-                y2_sb = ring.tile([P, width], F32, name="y2_sb")
-                nc.scalar.copy(y2_sb[:], y2[:])
-                y12 = ring.tile([P, width], F32, name="y12")
-                nc.vector.tensor_tensor(y12[:], pair[:, 0, :], y2_sb[:], ALU.mult)
-                y13.append(pair)
-                prod.append(y12)
+                banks.append(bank)
+            y2, y1, y3 = banks
+            y2_sb = ring.tile([P, tiles, STRIP], F32, name="y2_sb")
+            nc.scalar.copy(y2_sb[:], y2[:])
+            y12 = ring.tile([P, tiles, STRIP], F32, name="y12")
+            nc.vector.tensor_tensor(y12[:], y1[:], y2_sb[:], ALU.mult)
+            return y12, y3, starts[c] + c0
 
-            def add_and_store(n):
-                res = ring.tile([P, width], F32, name="res", bufs=6)
-                nc.vector.tensor_tensor(res[:], y13[n][:, 1, :], prod[n][:], ALU.add)
-                nc.sync.dma_start(out[P * n : P * (n + 1), starts[c] : starts[c] + width], res[:])
+        def add_and_store(y12, y3, j0):
+            res = ring.tile([P, tiles, STRIP], F32, name="res", bufs=4)
+            nc.vector.tensor_tensor(res[:], y3[:], y12[:], ALU.add)
+            nc.sync.dma_start(out.rearrange("(n p) j -> p n j", p=P)[:, :, j0 : j0 + STRIP], res[:])
 
-            tiles = N // P
-            for n in range(tiles + 1):
-                if n < tiles:
-                    multiply(n)
-                if n >= 1:
-                    add_and_store(n - 1)
+        def finish(c):
+            for c0 in range(0, CHUNKS[c], STRIP):
+                pending.append(multiply(c, c0))
+                if len(pending) == 2:
+                    add_and_store(*pending.pop(0))
 
-        for step in range(len(CHUNKS) + 2):
-            if step < len(CHUNKS):
-                make_z(step)
-            if 1 <= step <= len(CHUNKS):
-                quantise_z(step - 1)
-            if step >= 2:
-                finish(step - 2)
+        make_z(0)
+        make_z(1)
+        interleave_z(0)
+        interleave_z(1)
+        quantise_z(0)
+        make_z(2)
+        interleave_z(2)
+        quantise_z(1)
+        make_z(3)
+        interleave_z(3)
+        finish(0)
+        quantise_z(2)
+        finish(1)
+        quantise_z(3)
+        finish(2)
+        finish(3)
+        add_and_store(*pending.pop(0))

@@ -2,6 +2,7 @@ import math
 from contextlib import ExitStack
 
 import concourse.mybir as mybir
+from concourse.masks import make_identity
 
 K, K2, T, T2, S, SAMPLES, H, N = 1024, 512, 4096, 2048, 1024, 512, 512, 384
 FLOPS = 2 * (K * H * S + K2 * H * SAMPLES + 3 * H * N * S)
@@ -19,11 +20,21 @@ ACT = mybir.ActivationFunctionType
 
 P = 128
 PACK = 4
-QUADS = 4
-PASSES = K // (P * PACK)
+QUAD = 32
+QUADS = P // QUAD
+SCALE_ROWS = 4
+K_PASS = P * PACK
+PASSES = K // K_PASS
+LIST_ROWS = 16
 HALF = 512
-CHUNKS = (256, 256, 256, 256)
+PAIR = 2
+CHUNK = 256
+CHUNKS = S // CHUNK
+AHEAD = 2
 STRIP = 128
+ROW_TILES = N // P
+BANKS = 8
+QUAD_ORDER = (0, 2, 1, 3)
 
 
 def tile_list_trap_string_landings_kernel(
@@ -40,83 +51,73 @@ def tile_list_trap_string_landings_kernel(
         def held(shape, dtype, name):
             return keep.tile(shape, dtype, name=name, align_bytes=64)
 
-        def load_words(words, name):
-            tile = held([P, words.shape[1]], I32, name)
-            nc.sync.dma_start(tile[:], words.rearrange("p c i -> p (c i)").bitcast(I32))
-            return tile
-
-        def load_scale_rows(tile, scales, quad):
-            rows = scales.shape[0] * 4
-            nc.sync.dma_start(
-                tile[32 * quad : 32 * quad + rows, :].bitcast(I32),
-                scales[:, 4 * quad : 4 * quad + 4, :].bitcast(I32),
-            )
+        def next_bank(shape, name):
+            return psum.tile(shape, F32, name=name, tag="bank", bufs=BANKS)
 
         def load_list(src, name):
             tile = lists.tile(list(src.shape), U16, name=name)
             nc.sync.dma_start(tile[:], src)
             return tile
 
-        tab2_planes = held([P, T2], U8, "tab2_planes")
-        w2_planes = held([P, H], U8, "w2_planes")
-        tab_planes = held([P, T], U8, "tab_planes")
-        w5_planes = held([P, N], U8, "w5_planes")
-        v_planes = held([P, S], U8, "v_planes")
-        pages = [held([P, S], F32, "page%d" % t) for t in range(PACK)]
-        for planes in (tab2_planes, w2_planes, tab_planes):
-            nc.gpsimd.memset(planes[:].bitcast(I32), 0)
-        for page in pages[2:]:
-            nc.gpsimd.memset(page[:], 0.0)
-        nc.gpsimd.memset(w5_planes[:].bitcast(I32), 0)
-        seed = held([P, 16], F32, "seed")
-        nc.vector.memset(seed[:], 0.0)
-        warm = held([P, 16], F32, "warm")
-        nc.scalar.activation(warm[:], seed[:], ACT.Sin)
-        for page in pages[:2]:
-            nc.vector.memset(page[:], 0.0)
+        def load_words(words, name):
+            tile = held([P, words.shape[1]], I32, name)
+            nc.sync.dma_start(tile[:], words.rearrange("p c i -> p (c i)").bitcast(I32))
+            return tile
 
-        def load_wgs(t0, t1):
-            tile = held([P, t1 - t0, SAMPLES], F32, "wgs%d" % t0)
-            for quad in (0, 2, 1, 3):
+        def load_planes(tile, scales, quads):
+            rows = scales.shape[0] * SCALE_ROWS
+            for quad in quads:
                 nc.sync.dma_start(
-                    tile[32 * quad : 32 * quad + 32],
-                    wgs.rearrange("(q t) j -> q t j", t=PACK)[:, t0:t1, :],
+                    tile[QUAD * quad : QUAD * quad + rows, :].bitcast(I32),
+                    scales[:, SCALE_ROWS * quad : SCALE_ROWS * (quad + 1), :].bitcast(I32),
                 )
-            return [tile[:, t, :] for t in range(t1 - t0)]
 
         def load_rows(w, name):
             raw = held([P, PACK, w.shape[1]], F32, name)
             nc.sync.dma_start(raw[:], w.rearrange("(p i) c -> p i c", i=PACK))
             return raw
 
+        tab2_planes = held([P, T2], U8, "tab2_planes")
+        w2_planes = held([P, H], U8, "w2_planes")
+        tab_planes = held([P, T], U8, "tab_planes")
+        w5_planes = held([P, N], U8, "w5_planes")
+        pages = [held([P, S], F32, "page%d" % t) for t in range(PACK)]
+        for planes in (tab2_planes, w2_planes, tab_planes):
+            nc.gpsimd.memset(planes[:].bitcast(I32), 0)
+        identity = held([P, P], F32, "identity")
+        make_identity(nc, identity[:])
+        for page in pages[PACK // 2 :]:
+            nc.gpsimd.memset(page[:], 0.0)
+        nc.gpsimd.memset(w5_planes[:].bitcast(I32), 0)
+
+        angle = held([P, 1], F32, "angle")
+        nc.vector.memset(angle[:], 0.0)
+        no_bias = held([P, 1], F32, "no_bias")
+        nc.scalar.activation(no_bias[:], angle[:], ACT.Sin)
+        for page in pages[: PACK // 2]:
+            nc.vector.memset(page[:], 0.0)
+
         idx2 = load_list(offs2, "idx2")
         w2_raw = held([P, 2 * H], U8, "w2_raw")
         nc.sync.dma_start(w2_raw[:].bitcast(I32), w2_words[0].bitcast(I32))
         idx = load_list(offs, "idx")
-        for quad in (0, 2, 1, 3):
-            load_scale_rows(tab2_planes, tab2_scales, quad)
+        load_planes(tab2_planes, tab2_scales, QUAD_ORDER)
         tab2_sb = load_words(tab2_words[0], "tab2_sb")
-        for quad in (0, 2, 1, 3):
-            load_scale_rows(w2_planes, w2_scales, quad)
-        for quad in (0, 2, 1, 3):
-            load_scale_rows(tab_planes, tab_scales, quad)
+        wgs_raw = held([P, SAMPLES], F32, "wgs_raw")
+        nc.sync.dma_start(wgs_raw[:], wgs)
+        load_planes(w2_planes, w2_scales, QUAD_ORDER)
+        load_planes(tab_planes, tab_scales, QUAD_ORDER)
         places = load_list(pos1, "places")
-        wgs_sb, w1_raw = [], []
-        for a in range(PASSES):
-            wgs_sb.extend(load_wgs(2 * a, 2 * a + 2))
-            w1_raw.append(load_rows(w1[512 * a : 512 * (a + 1), :], "w1_raw%d" % a))
+        w1_raw = [load_rows(w1[K_PASS * a : K_PASS * (a + 1), :], "w1_raw%d" % a) for a in range(PASSES)]
         w46_raw = [load_rows(w4, "w4_raw"), load_rows(w6, "w6_raw")]
         tab_sb = [load_words(tab_words[a], "tab_sb%d" % a) for a in range(PASSES)]
         gain_sb = held([P, PACK], F32, "gain_sb")
         nc.sync.dma_start(gain_sb[:], gain.rearrange("(p t) -> p t", t=PACK))
-        gm_sb = []
+        gm_sb = [held([P, S], F32, "gm%d" % t) for t in range(PACK)]
         for t in range(PACK):
-            g = held([P, S], F32, "gm%d" % t)
-            nc.sync.dma_start(g[:], gm.rearrange("(p t) j -> p t j", t=PACK)[:, t, :])
-            gm_sb.append(g)
-        w5_sb = load_words(w5_words[0], "w5_sb")
-        for quad in range(QUADS):
-            load_scale_rows(w5_planes, w5_scales, quad)
+            nc.sync.dma_start(gm_sb[t][:], gm.rearrange("(p t) j -> p t j", t=PACK)[:, t, :])
+        w5_codes = load_words(w5_words[0], "w5_codes")
+        load_planes(w5_planes, w5_scales, range(QUADS))
 
         v2_planes = held([P, SAMPLES], U8, "v2_planes")
         nc.vector.tensor_copy(v2_planes[:], tab2_planes[:].indirect(idx2[:]))
@@ -127,35 +128,47 @@ def tile_list_trap_string_landings_kernel(
         )
         v2_codes = held([P, SAMPLES], U32, "v2_codes")
         nc.vector.tensor_copy(v2_codes[:], tab2_sb[:].bitcast(U32).indirect(idx2[:]))
-        w2_dealt = held([P, H], U8, "w2_dealt")
+        w2_dealt_planes = held([P, H], U8, "w2_dealt_planes")
         nc.vector.tensor_copy(
-            w2_dealt[:].rearrange("p (t m) -> p t m", t=PACK),
+            w2_dealt_planes[:].rearrange("p (t m) -> p t m", t=PACK),
             w2_planes[:].rearrange("p (m t) -> p t m", t=PACK),
         )
+
+        v_planes = held([P, S], U8, "v_planes")
         nc.vector.tensor_copy(v_planes[:], tab_planes[:].indirect(idx[:]))
-        b_sizes = []
+
+        blocks = SAMPLES // P
+        turned = next_bank([P, blocks, P], "turned")
+        for u in range(blocks):
+            nc.tensor.transpose(turned[:, u, :], wgs_raw[:, P * u : P * (u + 1)], identity[:])
+        b_slices, wgs_slices = [], []
         for t in range(PACK):
-            acc = psum.tile([P, SAMPLES], F32, name="acc", tag="bank", bufs=8)
+            spread = ring.tile([P, blocks, QUADS, QUAD], F32, name="spread")
+            picked = turned[:].rearrange("p u (q t) -> p u q t", t=PACK)[:, :, :, t]
+            nc.scalar.copy(spread[:], picked.unsqueeze(2).broadcast_to([P, blocks, QUADS, QUAD]))
+            back = next_bank([P, blocks, P], "back")
+            for u in range(blocks):
+                nc.tensor.transpose(back[:, u, :], spread[:, u].rearrange("p g q -> p (g q)"), identity[:])
+            wgs_slice = held([P, SAMPLES], F32, "wgs%d" % t)
+            nc.scalar.copy(wgs_slice[:], back[:].rearrange("p u j -> p (u j)"))
+            wgs_slices.append(wgs_slice)
+
+            b_sum = next_bank([P, SAMPLES], "b_sum")
             nc.tensor.matmul_mx(
-                out=acc[:],
+                out=b_sum[:],
                 lhsT=w2_codes[:, 2 * P * t : 2 * P * (t + 1)].bitcast(FP4X4),
-                lhsT_scale=w2_dealt[:, P * t : P * (t + 1)],
+                lhsT_scale=w2_dealt_planes[:, P * t : P * (t + 1)],
                 rhs=v2_codes[:].bitcast(FP8X4),
                 rhs_scale=v2_planes[:],
                 start=True,
                 stop=True,
             )
-            b_abs = held([P, SAMPLES], F32, "b_abs%d" % t)
-            nc.scalar.activation(b_abs[:], acc[:], ACT.Abs)
-            b_sizes.append(b_abs)
-
-        def place(t):
-            nc.vector.tensor_tensor(
-                pages[t][:].indirect(places[:]), b_sizes[t][:], wgs_sb[t], ALU.mult
-            )
+            b_slice = held([P, SAMPLES], F32, "b%d" % t)
+            nc.scalar.activation(b_slice[:], b_sum[:], ACT.Abs, bias=no_bias[:])
+            b_slices.append(b_slice)
 
         for t in range(PACK):
-            place(t)
+            nc.vector.tensor_tensor(pages[t][:].indirect(places[:]), b_slices[t][:], wgs_slices[t][:], ALU.mult)
 
         w1_codes, w1_planes = [], []
         for a in range(PASSES):
@@ -182,120 +195,121 @@ def tile_list_trap_string_landings_kernel(
                 in_=w46_grouped[:, c0:c1, :].rearrange("p c i -> p (c i)"),
             )
 
-        cosines = {}
+        cosines, waiting = {}, []
 
-        def take_cosine(h, t, size):
-            cosine = held([P, HALF], F32, "cos%d_%d" % (h, t))
-            nc.scalar.activation(cosine[:], size[:], ACT.Sin, bias=math.pi / 2, scale=-1.0)
-            cosines[h, t] = cosine
+        def take_cosine(c, g, magnitude):
+            cosine = held([P, PAIR, CHUNK], F32, "cos%d_%d" % (c, g))
+            nc.scalar.activation(cosine[:], magnitude[:], ACT.Sin, bias=math.pi / 2, scale=-1.0)
+            cosines[c, g] = cosine
 
         for h in range(S // HALF):
-            part = idx[:, h * HALF // 16 : (h + 1) * HALF // 16]
+            part = idx[:, h * HALF // LIST_ROWS : (h + 1) * HALF // LIST_ROWS]
             v_codes = []
             for a in range(PASSES):
                 codes = held([P, HALF], U32, "v_codes%d_%d" % (h, a))
                 nc.vector.tensor_copy(codes[:], tab_sb[a][:].bitcast(U32).indirect(part))
                 v_codes.append(codes)
-            for t in range(PACK):
-                acc = psum.tile([P, HALF], F32, name="acc", tag="bank", bufs=8)
-                for a in range(PASSES):
-                    nc.tensor.matmul_mx(
-                        out=acc[:],
-                        lhsT=w1_codes[a][:, P * t : P * (t + 1)].bitcast(FP8X4),
-                        lhsT_scale=w1_planes[a][:, P * t : P * (t + 1)],
-                        rhs=v_codes[a][:].bitcast(FP8X4),
-                        rhs_scale=v_planes[4 * a : P, h * HALF : (h + 1) * HALF],
-                        start=(a == 0),
-                        stop=(a == PASSES - 1),
-                    )
-                size = ring.tile([P, HALF], F32, name="size")
-                nc.scalar.activation(size[:], acc[:], ACT.Abs)
-                if t > 0:
-                    take_cosine(h, t - 1, last_size)
-                last_size = size
-            take_cosine(h, PACK - 1, last_size)
+            for c0 in range(0, HALF, CHUNK):
+                j0 = h * HALF + c0
+                for g in range(PACK // PAIR):
+                    a_sum = next_bank([P, PAIR, CHUNK], "a_sum")
+                    for e in range(PAIR):
+                        t = PAIR * g + e
+                        for a in range(PASSES):
+                            nc.tensor.matmul_mx(
+                                out=a_sum[:, e, :],
+                                lhsT=w1_codes[a][:, P * t : P * (t + 1)].bitcast(FP8X4),
+                                lhsT_scale=w1_planes[a][:, P * t : P * (t + 1)],
+                                rhs=v_codes[a][:, c0 : c0 + CHUNK].bitcast(FP8X4),
+                                rhs_scale=v_planes[SCALE_ROWS * a : P, j0 : j0 + CHUNK],
+                                start=(a == 0),
+                                stop=(a == PASSES - 1),
+                            )
+                    magnitude = ring.tile([P, PAIR, CHUNK], F32, name="magnitude")
+                    nc.scalar.activation(magnitude[:], a_sum[:], ACT.Abs, bias=no_bias[:])
+                    waiting.append((j0 // CHUNK, g, magnitude))
+                    if len(waiting) == 2:
+                        take_cosine(*waiting.pop(0))
+        take_cosine(*waiting.pop(0))
 
-        gated = []
         for t in range(PACK):
             nc.vector.tensor_tensor(gm_sb[t][:], pages[t][:], gm_sb[t][:], ALU.mult)
-            gated.append(gm_sb[t])
 
-        starts = [sum(CHUNKS[:c]) for c in range(len(CHUNKS))]
-        z_rows, z_grouped, z_q = {}, {}, {}
+        z_rows, z_grouped, z_quantised = {}, {}, {}
 
         def make_z(c):
-            width = CHUNKS[c]
-            h, c0 = divmod(starts[c], HALF)
-            rows = ring.tile([P, PACK, width], BF16, name="z_rows", bufs=4)
+            rows = ring.tile([P, PACK, CHUNK], BF16, name="z_rows", bufs=CHUNKS)
             for t in range(PACK):
                 nc.vector.scalar_tensor_tensor(
-                    rows[:, t, :], cosines[h, t][:, c0 : c0 + width], gain_sb[:, t : t + 1],
-                    gated[t][:, starts[c] : starts[c] + width], ALU.mult, ALU.add,
+                    rows[:, t, :], cosines[c, t // PAIR][:, t % PAIR, :], gain_sb[:, t : t + 1],
+                    gm_sb[t][:, c * CHUNK : (c + 1) * CHUNK], ALU.mult, ALU.add,
                 )
             z_rows[c] = rows
 
         def interleave_z(c):
-            grouped = ring.tile([P, CHUNKS[c], PACK], BF16, name="z_grouped", align_bytes=64, bufs=4)
-            copy = nc.vector.tensor_copy if starts[c] < HALF else nc.scalar.copy
+            grouped = ring.tile([P, CHUNK, PACK], BF16, name="z_grouped", align_bytes=64, bufs=CHUNKS)
+            copy = nc.vector.tensor_copy if c == 0 else nc.scalar.copy
             copy(grouped[:], z_rows[c][:].rearrange("p t c -> p c t"))
             z_grouped[c] = grouped
 
         def quantise_z(c):
-            codes = ring.tile([P, CHUNKS[c]], U32, name="z_codes", align_bytes=64, bufs=4)
-            planes = ring.tile([P, CHUNKS[c]], U8, name="z_planes", align_bytes=64, bufs=4)
+            codes = ring.tile([P, CHUNK], U32, name="z_codes", align_bytes=64, bufs=CHUNKS)
+            planes = ring.tile([P, CHUNK], U8, name="z_planes", align_bytes=64, bufs=CHUNKS)
             nc.vector.quantize_mx(
                 out=codes[:].bitcast(FP8X4), scales=planes[:], in_=z_grouped[c][:].rearrange("p c t -> p (c t)")
             )
-            z_q[c] = (codes, planes)
-
-        tiles = N // P
-        pending = []
+            z_quantised[c] = (codes, planes)
 
         def multiply(c, c0):
-            codes, planes = z_q[c]
+            codes, planes = z_quantised[c]
             cols = slice(c0, c0 + STRIP)
             banks = []
-            for w_codes, w_planes, first in ((w5_sb, w5_planes, 0), (w46_codes, w46_planes, 0), (w46_codes, w46_planes, N)):
-                bank = psum.tile([P, tiles, STRIP], F32, name="y", tag="bank", bufs=8)
-                for n in range(tiles):
+            for w_codes, w_planes, first in (
+                (w5_codes, w5_planes, 0), (w46_codes, w46_planes, 0), (w46_codes, w46_planes, N)
+            ):
+                bank = next_bank([P, ROW_TILES, STRIP], "y")
+                for n in range(ROW_TILES):
                     w_cols = slice(first + P * n, first + P * (n + 1))
                     nc.tensor.matmul_mx(
-                        out=bank[:, n, :], lhsT=w_codes[:, w_cols].bitcast(FP8X4), lhsT_scale=w_planes[:, w_cols],
-                        rhs=codes[:, cols].bitcast(FP8X4), rhs_scale=planes[:, cols], start=True, stop=True,
+                        out=bank[:, n, :],
+                        lhsT=w_codes[:, w_cols].bitcast(FP8X4),
+                        lhsT_scale=w_planes[:, w_cols],
+                        rhs=codes[:, cols].bitcast(FP8X4),
+                        rhs_scale=planes[:, cols],
+                        start=True,
+                        stop=True,
                     )
                 banks.append(bank)
             y2, y1, y3 = banks
-            y2_sb = ring.tile([P, tiles, STRIP], F32, name="y2_sb")
+            y2_sb = ring.tile([P, ROW_TILES, STRIP], F32, name="y2_sb")
             nc.scalar.copy(y2_sb[:], y2[:])
-            y12 = ring.tile([P, tiles, STRIP], F32, name="y12")
+            y12 = ring.tile([P, ROW_TILES, STRIP], F32, name="y12")
             nc.vector.tensor_tensor(y12[:], y1[:], y2_sb[:], ALU.mult)
-            return y12, y3, starts[c] + c0
+            return y12, y3, c * CHUNK + c0
 
         def add_and_store(y12, y3, j0):
-            res = ring.tile([P, tiles, STRIP], F32, name="res", bufs=4)
-            nc.vector.tensor_tensor(res[:], y3[:], y12[:], ALU.add)
-            nc.sync.dma_start(out.rearrange("(n p) j -> p n j", p=P)[:, :, j0 : j0 + STRIP], res[:])
+            result = ring.tile([P, ROW_TILES, STRIP], F32, name="result", bufs=4)
+            nc.vector.tensor_tensor(result[:], y3[:], y12[:], ALU.add)
+            nc.sync.dma_start(out.rearrange("(n p) j -> p n j", p=P)[:, :, j0 : j0 + STRIP], result[:])
+
+        unsummed = []
 
         def finish(c):
-            for c0 in range(0, CHUNKS[c], STRIP):
-                pending.append(multiply(c, c0))
-                if len(pending) == 2:
-                    add_and_store(*pending.pop(0))
+            for c0 in range(0, CHUNK, STRIP):
+                unsummed.append(multiply(c, c0))
+                if len(unsummed) == 2:
+                    add_and_store(*unsummed.pop(0))
 
-        make_z(0)
-        make_z(1)
-        interleave_z(0)
-        interleave_z(1)
-        quantise_z(0)
-        make_z(2)
-        interleave_z(2)
-        quantise_z(1)
-        make_z(3)
-        interleave_z(3)
-        finish(0)
-        quantise_z(2)
-        finish(1)
-        quantise_z(3)
-        finish(2)
-        finish(3)
-        add_and_store(*pending.pop(0))
+        for c in range(AHEAD):
+            make_z(c)
+        for c in range(AHEAD):
+            interleave_z(c)
+        for c in range(AHEAD):
+            make_z(c + AHEAD)
+            quantise_z(c)
+        for c in range(CHUNKS):
+            finish(c)
+            if c + AHEAD < CHUNKS:
+                interleave_z(c + AHEAD)
+                quantise_z(c + AHEAD)
+        add_and_store(*unsummed.pop(0))

import math
from contextlib import ExitStack

import concourse.mybir as mybir
from concourse.masks import make_identity

K, K2, T, T2, S, SAMPLES, H, N = 1024, 512, 4096, 2048, 1024, 512, 512, 384
FLOPS = 2 * (K * H * S + K2 * H * SAMPLES + 3 * H * N * S)

F32 = mybir.dt.float32
BF16 = mybir.dt.bfloat16
I32 = mybir.dt.int32
U32 = mybir.dt.uint32
U16 = mybir.dt.uint16
U8 = mybir.dt.uint8
FP8X4 = mybir.dt.float8_e4m3fn_x4
FP4X4 = mybir.dt.float4_e2m1fn_x4
ALU = mybir.AluOpType
ACT = mybir.ActivationFunctionType

P = 128
PACK = 4
QUAD = 32
QUADS = P // QUAD
SCALE_ROWS = 4
K_PASS = P * PACK
PASSES = K // K_PASS
LIST_ROWS = 16
HALF = 512
PAIR = 2
CHUNK = 256
CHUNKS = S // CHUNK
AHEAD = 2
STRIP = 128
ROW_TILES = N // P
BANKS = 8
QUAD_ORDER = (0, 2, 1, 3)


def tile_list_trap_string_landings_kernel(
    tc, tab_words, tab_scales, tab2_words, tab2_scales, offs, offs2, pos1, w1, gain,
    w2_words, w2_scales, wgs, gm, w4, w5_words, w5_scales, w6, out,
):
    nc = tc.nc
    with ExitStack() as ctx:
        lists = ctx.enter_context(tc.tile_pool(name="lists", bufs=1))
        keep = ctx.enter_context(tc.tile_pool(name="keep", bufs=1))
        ring = ctx.enter_context(tc.tile_pool(name="ring", bufs=3))
        psum = ctx.enter_context(tc.psum_pool(name="psum", bufs=1))

        def held(shape, dtype, name):
            return keep.tile(shape, dtype, name=name, align_bytes=64)

        def next_bank(shape, name):
            return psum.tile(shape, F32, name=name, tag="bank", bufs=BANKS)

        def load_list(src, name):
            tile = lists.tile(list(src.shape), U16, name=name)
            nc.sync.dma_start(tile[:], src)
            return tile

        def load_words(words, name):
            tile = held([P, words.shape[1]], I32, name)
            nc.sync.dma_start(tile[:], words.rearrange("p c i -> p (c i)").bitcast(I32))
            return tile

        def load_planes(tile, scales, quads):
            rows = scales.shape[0] * SCALE_ROWS
            for quad in quads:
                nc.sync.dma_start(
                    tile[QUAD * quad : QUAD * quad + rows, :].bitcast(I32),
                    scales[:, SCALE_ROWS * quad : SCALE_ROWS * (quad + 1), :].bitcast(I32),
                )

        def load_rows(w, name):
            raw = held([P, PACK, w.shape[1]], F32, name)
            nc.sync.dma_start(raw[:], w.rearrange("(p i) c -> p i c", i=PACK))
            return raw

        tab2_planes = held([P, T2], U8, "tab2_planes")
        w2_planes = held([P, H], U8, "w2_planes")
        tab_planes = held([P, T], U8, "tab_planes")
        w5_planes = held([P, N], U8, "w5_planes")
        pages = [held([P, S], F32, "page%d" % t) for t in range(PACK)]
        for planes in (tab2_planes, w2_planes, tab_planes):
            nc.gpsimd.memset(planes[:].bitcast(I32), 0)
        identity = held([P, P], F32, "identity")
        make_identity(nc, identity[:])
        for page in pages[PACK // 2 :]:
            nc.gpsimd.memset(page[:], 0.0)
        nc.gpsimd.memset(w5_planes[:].bitcast(I32), 0)

        angle = held([P, 1], F32, "angle")
        nc.vector.memset(angle[:], 0.0)
        no_bias = held([P, 1], F32, "no_bias")
        nc.scalar.activation(no_bias[:], angle[:], ACT.Sin)
        for page in pages[: PACK // 2]:
            nc.vector.memset(page[:], 0.0)

        idx2 = load_list(offs2, "idx2")
        w2_raw = held([P, 2 * H], U8, "w2_raw")
        nc.sync.dma_start(w2_raw[:].bitcast(I32), w2_words[0].bitcast(I32))
        idx = load_list(offs, "idx")
        load_planes(tab2_planes, tab2_scales, QUAD_ORDER)
        tab2_sb = load_words(tab2_words[0], "tab2_sb")
        wgs_raw = held([P, SAMPLES], F32, "wgs_raw")
        nc.sync.dma_start(wgs_raw[:], wgs)
        load_planes(w2_planes, w2_scales, QUAD_ORDER)
        load_planes(tab_planes, tab_scales, QUAD_ORDER)
        places = load_list(pos1, "places")
        w1_raw = [load_rows(w1[K_PASS * a : K_PASS * (a + 1), :], "w1_raw%d" % a) for a in range(PASSES)]
        w46_raw = [load_rows(w4, "w4_raw"), load_rows(w6, "w6_raw")]
        tab_sb = [load_words(tab_words[a], "tab_sb%d" % a) for a in range(PASSES)]
        gain_sb = held([P, PACK], F32, "gain_sb")
        nc.sync.dma_start(gain_sb[:], gain.rearrange("(p t) -> p t", t=PACK))
        gm_sb = [held([P, S], F32, "gm%d" % t) for t in range(PACK)]
        for t in range(PACK):
            nc.sync.dma_start(gm_sb[t][:], gm.rearrange("(p t) j -> p t j", t=PACK)[:, t, :])
        w5_codes = load_words(w5_words[0], "w5_codes")
        load_planes(w5_planes, w5_scales, range(QUADS))

        v2_planes = held([P, SAMPLES], U8, "v2_planes")
        nc.vector.tensor_copy(v2_planes[:], tab2_planes[:].indirect(idx2[:]))
        w2_codes = held([P, 2 * H], U8, "w2_codes")
        nc.vector.tensor_copy(
            w2_codes[:].rearrange("p (t m e) -> p t m e", t=PACK, e=2),
            w2_raw[:].rearrange("p (m t e) -> p t m e", t=PACK, e=2),
        )
        v2_codes = held([P, SAMPLES], U32, "v2_codes")
        nc.vector.tensor_copy(v2_codes[:], tab2_sb[:].bitcast(U32).indirect(idx2[:]))
        w2_dealt_planes = held([P, H], U8, "w2_dealt_planes")
        nc.vector.tensor_copy(
            w2_dealt_planes[:].rearrange("p (t m) -> p t m", t=PACK),
            w2_planes[:].rearrange("p (m t) -> p t m", t=PACK),
        )

        v_planes = held([P, S], U8, "v_planes")
        nc.vector.tensor_copy(v_planes[:], tab_planes[:].indirect(idx[:]))

        blocks = SAMPLES // P
        turned = next_bank([P, blocks, P], "turned")
        for u in range(blocks):
            nc.tensor.transpose(turned[:, u, :], wgs_raw[:, P * u : P * (u + 1)], identity[:])
        b_slices, wgs_slices = [], []
        for t in range(PACK):
            spread = ring.tile([P, blocks, QUADS, QUAD], F32, name="spread")
            picked = turned[:].rearrange("p u (q t) -> p u q t", t=PACK)[:, :, :, t]
            nc.scalar.copy(spread[:], picked.unsqueeze(2).broadcast_to([P, blocks, QUADS, QUAD]))
            back = next_bank([P, blocks, P], "back")
            for u in range(blocks):
                nc.tensor.transpose(back[:, u, :], spread[:, u].rearrange("p g q -> p (g q)"), identity[:])
            wgs_slice = held([P, SAMPLES], F32, "wgs%d" % t)
            nc.scalar.copy(wgs_slice[:], back[:].rearrange("p u j -> p (u j)"))
            wgs_slices.append(wgs_slice)

            b_sum = next_bank([P, SAMPLES], "b_sum")
            nc.tensor.matmul_mx(
                out=b_sum[:],
                lhsT=w2_codes[:, 2 * P * t : 2 * P * (t + 1)].bitcast(FP4X4),
                lhsT_scale=w2_dealt_planes[:, P * t : P * (t + 1)],
                rhs=v2_codes[:].bitcast(FP8X4),
                rhs_scale=v2_planes[:],
                start=True,
                stop=True,
            )
            b_slice = held([P, SAMPLES], F32, "b%d" % t)
            nc.scalar.activation(b_slice[:], b_sum[:], ACT.Abs, bias=no_bias[:])
            b_slices.append(b_slice)

        for t in range(PACK):
            nc.vector.tensor_tensor(pages[t][:].indirect(places[:]), b_slices[t][:], wgs_slices[t][:], ALU.mult)

        w1_codes, w1_planes = [], []
        for a in range(PASSES):
            grouped = held([P, H * PACK], BF16, "w1_grouped%d" % a)
            nc.scalar.copy(
                grouped[:].rearrange("p (t m i) -> p m t i", t=PACK, i=PACK),
                w1_raw[a][:].rearrange("p i (m t) -> p m t i", t=PACK),
            )
            codes = held([P, H], U32, "w1_codes%d" % a)
            planes = held([P, H], U8, "w1_planes%d" % a)
            nc.vector.quantize_mx(out=codes[:].bitcast(FP8X4), scales=planes[:], in_=grouped[:])
            w1_codes.append(codes)
            w1_planes.append(planes)

        w46_grouped = held([P, 2 * N, PACK], BF16, "w46_grouped")
        for u in range(2):
            nc.scalar.copy(w46_grouped[:, N * u : N * (u + 1), :], w46_raw[u][:].rearrange("p i c -> p c i"))
        w46_codes = held([P, 2 * N], U32, "w46_codes")
        w46_planes = held([P, 2 * N], U8, "w46_planes")
        for c0, c1 in ((0, 512), (512, 2 * N)):
            nc.vector.quantize_mx(
                out=w46_codes[:, c0:c1].bitcast(FP8X4),
                scales=w46_planes[:, c0:c1],
                in_=w46_grouped[:, c0:c1, :].rearrange("p c i -> p (c i)"),
            )

        cosines, waiting = {}, []

        def take_cosine(c, g, magnitude):
            cosine = held([P, PAIR, CHUNK], F32, "cos%d_%d" % (c, g))
            nc.scalar.activation(cosine[:], magnitude[:], ACT.Sin, bias=math.pi / 2, scale=-1.0)
            cosines[c, g] = cosine

        for h in range(S // HALF):
            part = idx[:, h * HALF // LIST_ROWS : (h + 1) * HALF // LIST_ROWS]
            v_codes = []
            for a in range(PASSES):
                codes = held([P, HALF], U32, "v_codes%d_%d" % (h, a))
                nc.vector.tensor_copy(codes[:], tab_sb[a][:].bitcast(U32).indirect(part))
                v_codes.append(codes)
            for c0 in range(0, HALF, CHUNK):
                j0 = h * HALF + c0
                for g in range(PACK // PAIR):
                    a_sum = next_bank([P, PAIR, CHUNK], "a_sum")
                    for e in range(PAIR):
                        t = PAIR * g + e
                        for a in range(PASSES):
                            nc.tensor.matmul_mx(
                                out=a_sum[:, e, :],
                                lhsT=w1_codes[a][:, P * t : P * (t + 1)].bitcast(FP8X4),
                                lhsT_scale=w1_planes[a][:, P * t : P * (t + 1)],
                                rhs=v_codes[a][:, c0 : c0 + CHUNK].bitcast(FP8X4),
                                rhs_scale=v_planes[SCALE_ROWS * a : P, j0 : j0 + CHUNK],
                                start=(a == 0),
                                stop=(a == PASSES - 1),
                            )
                    magnitude = ring.tile([P, PAIR, CHUNK], F32, name="magnitude")
                    nc.scalar.activation(magnitude[:], a_sum[:], ACT.Abs, bias=no_bias[:])
                    waiting.append((j0 // CHUNK, g, magnitude))
                    if len(waiting) == 2:
                        take_cosine(*waiting.pop(0))
        take_cosine(*waiting.pop(0))

        for t in range(PACK):
            nc.vector.tensor_tensor(gm_sb[t][:], pages[t][:], gm_sb[t][:], ALU.mult)

        z_rows, z_grouped, z_quantised = {}, {}, {}

        def make_z(c):
            rows = ring.tile([P, PACK, CHUNK], BF16, name="z_rows", bufs=CHUNKS)
            for t in range(PACK):
                nc.vector.scalar_tensor_tensor(
                    rows[:, t, :], cosines[c, t // PAIR][:, t % PAIR, :], gain_sb[:, t : t + 1],
                    gm_sb[t][:, c * CHUNK : (c + 1) * CHUNK], ALU.mult, ALU.add,
                )
            z_rows[c] = rows

        def interleave_z(c):
            grouped = ring.tile([P, CHUNK, PACK], BF16, name="z_grouped", align_bytes=64, bufs=CHUNKS)
            copy = nc.vector.tensor_copy if c == 0 else nc.scalar.copy
            copy(grouped[:], z_rows[c][:].rearrange("p t c -> p c t"))
            z_grouped[c] = grouped

        def quantise_z(c):
            codes = ring.tile([P, CHUNK], U32, name="z_codes", align_bytes=64, bufs=CHUNKS)
            planes = ring.tile([P, CHUNK], U8, name="z_planes", align_bytes=64, bufs=CHUNKS)
            nc.vector.quantize_mx(
                out=codes[:].bitcast(FP8X4), scales=planes[:], in_=z_grouped[c][:].rearrange("p c t -> p (c t)")
            )
            z_quantised[c] = (codes, planes)

        def multiply(c, c0):
            codes, planes = z_quantised[c]
            cols = slice(c0, c0 + STRIP)
            banks = []
            for w_codes, w_planes, first in (
                (w5_codes, w5_planes, 0), (w46_codes, w46_planes, 0), (w46_codes, w46_planes, N)
            ):
                bank = next_bank([P, ROW_TILES, STRIP], "y")
                for n in range(ROW_TILES):
                    w_cols = slice(first + P * n, first + P * (n + 1))
                    nc.tensor.matmul_mx(
                        out=bank[:, n, :],
                        lhsT=w_codes[:, w_cols].bitcast(FP8X4),
                        lhsT_scale=w_planes[:, w_cols],
                        rhs=codes[:, cols].bitcast(FP8X4),
                        rhs_scale=planes[:, cols],
                        start=True,
                        stop=True,
                    )
                banks.append(bank)
            y2, y1, y3 = banks
            y2_sb = ring.tile([P, ROW_TILES, STRIP], F32, name="y2_sb")
            nc.scalar.copy(y2_sb[:], y2[:])
            y12 = ring.tile([P, ROW_TILES, STRIP], F32, name="y12")
            nc.vector.tensor_tensor(y12[:], y1[:], y2_sb[:], ALU.mult)
            return y12, y3, c * CHUNK + c0

        def add_and_store(y12, y3, j0):
            result = ring.tile([P, ROW_TILES, STRIP], F32, name="result", bufs=4)
            nc.vector.tensor_tensor(result[:], y3[:], y12[:], ALU.add)
            nc.sync.dma_start(out.rearrange("(n p) j -> p n j", p=P)[:, :, j0 : j0 + STRIP], result[:])

        unsummed = []

        def finish(c):
            for c0 in range(0, CHUNK, STRIP):
                unsummed.append(multiply(c, c0))
                if len(unsummed) == 2:
                    add_and_store(*unsummed.pop(0))

        for c in range(AHEAD):
            make_z(c)
        for c in range(AHEAD):
            interleave_z(c)
        for c in range(AHEAD):
            make_z(c + AHEAD)
            quantise_z(c)
        for c in range(CHUNKS):
            finish(c)
            if c + AHEAD < CHUNKS:
                interleave_z(c + AHEAD)
                quantise_z(c + AHEAD)
        add_and_store(*unsummed.pop(0))
